import numpy as np, ml_dtypes
CORES = [16,23,24,31,64,71]
N = 6
NB, TK, FT = 8, 256, 1
def setup_inputs(rng):
    return {"x": rng.standard_normal((N, NB, 128, TK), dtype=np.float32).astype(ml_dtypes.bfloat16), "w1": (rng.standard_normal((N, 128, FT * 128), dtype=np.float32) / 8).astype(ml_dtypes.bfloat16), "w2": (rng.standard_normal((N, 128, FT * 128), dtype=np.float32) / np.float32(8 * np.sqrt(FT))).astype(ml_dtypes.bfloat16)}
def setup_inputs_big(rng):
    d = setup_inputs(rng)
    for k in ("x",): d[k] = (d[k].astype(np.float32) * 1048576.0).astype(d[k].dtype)
    return d
def setup_inputs_small(rng):
    d = setup_inputs(rng)
    for k in ("x",): d[k] = (d[k].astype(np.float32) * (1 / 1048576.0)).astype(d[k].dtype)
    return d
def reference(x, w1, w2):
    W1, W2 = w1.astype(np.float64), w2.astype(np.float64)
    a = x[0].astype(np.float64)
    for s in range(N):
        a = sum(np.einsum("kf,bkn->bfn", W2[s][:, 128 * f:128 * f + 128], np.maximum(np.einsum("kf,bkn->bfn", W1[s][:, 128 * f:128 * f + 128], a), 0.0)) for f in range(FT))
    y = np.full(x.shape, np.nan, ml_dtypes.bfloat16)
    y[N - 1] = a.astype(ml_dtypes.bfloat16)
    return {"y": y}

@@ -1,0 +1,272 @@
+from concourse.bass import DstId, RemoteDMATransfer
+from concourse.mybir import AluOpType
+
+NR, NB, TK = 6, 8, 256
+LAST = 6
+
+GROUPS = [(0, 0, 2), (1, 2, 2), (0, 4, 2), (1, 6, 1), (0, 7, 1)]
+PRE = {0: 2, 1: 1}
+MERGE_BANK = {0: 4, 1: 5, 3: 6, 4: 7, 2: 4}
+
+SCRATCH = {
+    "wt": ("sbuf", [128, NR * 256], "bfloat16"),
+    "xin": ("sbuf", [128, NB * TK], "bfloat16"),
+    "hin": ("sbuf", [128, NB * TK], "bfloat16"),
+    "ha": ("sbuf", [128, NB * TK], "bfloat16"),
+    "hb": ("sbuf", [128, NB * TK], "bfloat16"),
+    "yin": ("sbuf", [128, NB * TK], "bfloat16"),
+    "zeros": ("sbuf", [128, TK], "float32"),
+    "idsrc": ("sbuf", [128, 129], "bfloat16"),
+    "idd": ("dram", [129 * 128], "bfloat16"),
+    "ident": ("sbuf", [128, 128], "bfloat16"),
+    "wtr": ("sbuf", [128, 5 * 128], "bfloat16"),
+    "cm": ("sbuf", [128, 5 * 128], "bfloat16"),
+}
+for _b in range(8):
+    SCRATCH["ps%d" % _b] = ("psum", [128, 512], "float32")
+
+SEMAPHORES = (["w%d" % s for s in range(NR)] + ["x%d" % m for m in range(NB)] + ["u%d" % i for i in range(NB)]
+              + ["m%d" % s for s in range(5)] + ["a%d" % k for k in range(len(GROUPS))]
+              + ["r%d" % k for k in range(len(GROUPS))] + ["zs", "ids", "id1", "id2", "snd", "sts", "stc"])
+
+
+def _pick(mask, n):
+    out, b, c = 0, 0, 0
+    while c < n:
+        if (mask >> b) & 1:
+            out |= 1 << b
+            c += 1
+        b += 1
+    return out
+
+
+def _count(mask):
+    return bin(mask).count("1")
+
+
+def rank_program(g, core, T, topo):
+    rank = T.rank_of(core)
+    if rank is None:
+        return
+    cores = list(T.cores)
+    sink = cores[NR - 1]
+    helper = [c for c in cores if c != sink and topo.chip(c) == topo.chip(sink)][0]
+    lanes = [sink, helper]
+
+    waited = {}
+
+    def wait(q, qn, name, val):
+        if waited.get((qn, name), 0) >= val:
+            return
+        waited[(qn, name)] = val
+        q.wait_ge(T.sem[name], val)
+
+    sent = [0]
+
+    def engines(src, dsts, n=None):
+        m = topo.mask(src, dsts[0])
+        for d in dsts[1:]:
+            m &= topo.mask(src, d)
+        return m if n is None else _pick(m, min(n, _count(m)))
+
+    def send(dsts, ap, sem, n=None):
+        m = engines(core, dsts, n)
+        if len(dsts) == 1:
+            rid, pid, _ = topo.addr(dsts[0])
+            g.remote_dma(ap, ap, T.sem[sem], T.sem.snd, pid, rid, m)
+        else:
+            ids = [DstId(rid=topo.addr(d)[0], pnc=topo.addr(d)[1]) for d in dsts]
+            g.remote_dma_fused([RemoteDMATransfer(dst_ids=ids, dma_engine_mask=m, remote_sem=T.sem[sem], srcs=[ap],
+                                                  dsts=[ap for _ in dsts])], local_sem=T.sem.snd)
+        sent[0] += _count(m)
+
+    def route(s):
+        o = cores[s]
+        direct = [l for l in lanes if l != o and topo.may_write(o, l)]
+        blocked = [l for l in lanes if l != o and not topo.may_write(o, l)]
+        relay = None
+        if blocked:
+            near = [c for c in cores if c != o and topo.chip(c) == topo.chip(o)
+                    and all(topo.may_write(c, l) for l in blocked)]
+            relay = near[0]
+        return o, direct, blocked, relay
+
+    def wcols(s):
+        return T.wt[:, s * 256 + 128:(s + 1) * 256] if s == 0 else T.wt[:, s * 256:(s + 1) * 256]
+
+    def n_direct(o, direct):
+        return _count(engines(o, direct))
+
+    def n_relay_in(o, relay):
+        return _count(engines(o, [relay], 8))
+
+    def w_val(c, s):
+        o, direct, blocked, relay = route(s)
+        if c == o:
+            return 32
+        if c in direct:
+            return n_direct(o, direct)
+        if c == relay:
+            return n_relay_in(o, relay)
+        return _count(engines(relay, [c]))
+
+    g.sync.dma_start(T.wt[:, rank * 256:rank * 256 + 128], T.w1[:, :]).then_inc(T.sem["w%d" % rank], 16)
+    g.scalar.dma_start(T.wt[:, rank * 256 + 128:rank * 256 + 256], T.w2[:, :]).then_inc(T.sem["w%d" % rank], 16)
+
+    o, direct, blocked, relay = route(rank)
+    wait(g, "g", "w%d" % rank, 32)
+    if direct:
+        send(direct, wcols(rank), "w%d" % rank)
+    if blocked:
+        send([relay], wcols(rank), "w%d" % rank, 8)
+    for s in range(NR):
+        o2, d2, b2, r2 = route(s)
+        if r2 == core:
+            wait(g, "g", "w%d" % s, w_val(core, s))
+            for l in b2:
+                send([l], wcols(s), "w%d" % s)
+
+    banks = [T["ps%d" % b] for b in range(8)]
+
+    if rank == 0:
+        g.vector.memset(T.zeros[:, :], 0.0).then_inc(T.sem.zs, 1)
+        wait(g.vector, "v", "zs", 1)
+        for m in range(NB):
+            q = g.sync if m % 2 == 0 else g.scalar
+            q.dma_start(T.xin[:, m * TK:(m + 1) * TK], T.x[m]).then_inc(T.sem["x%d" % m], 16)
+        wait(g.tensor, "t", "w0", 32)
+        for m in range(NB):
+            wait(g.tensor, "t", "x%d" % m, 16)
+            g.tensor.matmul(out=banks[m][:, 0:TK], lhsT=T.wt[:, 0:128], rhs=T.xin[:, m * TK:(m + 1) * TK],
+                            start=True, stop=True).then_inc(T.sem["u%d" % m], 1)
+            wait(g.vector, "v", "u%d" % m, 1)
+            g.vector.tensor_tensor(out=T.hin[:, m * TK:(m + 1) * TK], in0=banks[m][:, 0:TK], in1=T.zeros[:, :],
+                                   op=AluOpType.max).then_inc(T.sem["u%d" % m], 1)
+        for k, (ln, b0, nb) in enumerate(GROUPS):
+            for m in range(b0, b0 + nb):
+                wait(g, "g", "u%d" % m, 2)
+            send([lanes[ln]], T.hin[:, b0 * TK:(b0 + nb) * TK], "a%d" % k)
+
+    if core in lanes:
+        ln = lanes.index(core)
+        src0 = cores[0]
+        waves, i = [], 0
+        for k, (l2, b0, nb) in enumerate(GROUPS):
+            if l2 != ln:
+                continue
+            if nb == 1:
+                cuts = [(b0 * TK, TK // 2), (b0 * TK + TK // 2, TK // 2)]
+            else:
+                cuts = [((b0 + j) * TK, TK) for j in range(nb)]
+            wave = []
+            for (c0, wd) in cuts:
+                wave.append((i, c0, wd, k))
+                i += 1
+            waves.append((k, b0, nb, wave))
+        pre = PRE[ln]
+
+        g.vector.memset(T.idsrc[:, :], 0.0).then_inc(T.sem.ids, 1)
+        wait(g.vector, "v", "ids", 1)
+        g.vector.memset(T.idsrc[:, 0:1], 1.0).then_inc(T.sem.ids, 1)
+        g.vector.memset(T.zeros[:, :], 0.0).then_inc(T.sem.zs, 1)
+        wait(g.vector, "v", "zs", 1)
+        wait(g.sync, "s", "ids", 2)
+        g.sync.dma_start(T.idd[:], T.idsrc[:, :]).then_inc(T.sem.id1, 16)
+        wait(g.sync, "s", "id1", 16)
+        g.sync.dma_start(T.ident[:, :], T.idd[0:128 * 128]).then_inc(T.sem.id2, 16)
+
+        def stages(wave, ks):
+            return [("S", u, k) for k in ks for u in wave]
+
+        w0 = waves[0][3]
+        head = [("T", 4), ("T", 0), ("T", 1), ("C", 4), ("C", 0)] + stages(w0, [1]) + [("T", 3), ("C", 3)]
+        for wv in waves[1:pre]:
+            head += stages(wv[3], [1])
+        tail = [("S", u, 2) for u in w0[1:]] + [("C", 2)] + stages(w0, range(3, LAST + 1))
+        for j, wv in enumerate(waves[1:], 1):
+            tail += stages(wv[3], range(2 if j < pre else 1, LAST + 1))
+        pe_ops = head + [("C", 1), ("T", 2), ("S", w0[0], 2)] + tail
+        ve_ops = head + [("C", 1), ("S", w0[0], 2), ("T", 2)] + tail
+
+        def hbuf(k):
+            return T.hin if k == 0 else (T.yin if k == LAST else (T.ha if k % 2 else T.hb))
+
+        pe, ve = g.tensor, g.vector
+        for op in pe_ops:
+            if op[0] == "T":
+                s = op[1]
+                wait(pe, "t", "id2", 16)
+                wait(pe, "t", "w%d" % s, w_val(core, s))
+                if s == 2:
+                    wait(pe, "t", "m0", 4)
+                pe.matmul(out=banks[MERGE_BANK[s]][:, 0:128], lhsT=T.wt[:, s * 256 + 128:s * 256 + 256],
+                          rhs=T.ident[:, :], start=True, stop=True).then_inc(T.sem["m%d" % s], 1)
+            elif op[0] == "C":
+                s = op[1]
+                wait(pe, "t", "m%d" % s, 2)
+                wait(pe, "t", "w%d" % (s + 1), w_val(core, s + 1))
+                pe.matmul(out=banks[MERGE_BANK[s]][:, 128:256], lhsT=T.wtr[:, s * 128:(s + 1) * 128],
+                          rhs=T.wt[:, (s + 1) * 256:(s + 1) * 256 + 128], start=True, stop=True
+                          ).then_inc(T.sem["m%d" % s], 1)
+            else:
+                (i, c0, wd, k), st = op[1], op[2]
+                if st == 1:
+                    wait(pe, "t", "a%d" % k, _count(engines(src0, [core])))
+                    if i >= 4:
+                        wait(pe, "t", "u%d" % (i - 4), 2 * LAST)
+                else:
+                    wait(pe, "t", "u%d" % i, 2 * (st - 1))
+                if st < LAST:
+                    wait(pe, "t", "m%d" % (st - 1), 4)
+                    lhsT = T.cm[:, (st - 1) * 128:st * 128]
+                else:
+                    wait(pe, "t", "w%d" % (NR - 1), w_val(core, NR - 1))
+                    lhsT = T.wt[:, (NR - 1) * 256 + 128:NR * 256]
+                pe.matmul(out=banks[i % 4][:, 0:wd], lhsT=lhsT, rhs=hbuf(st - 1)[:, c0:c0 + wd], start=True, stop=True
+                          ).then_inc(T.sem["u%d" % i], 1)
+        for op in ve_ops:
+            if op[0] == "T":
+                s = op[1]
+                wait(ve, "v", "m%d" % s, 1)
+                ve.tensor_copy(out=T.wtr[:, s * 128:(s + 1) * 128], in_=banks[MERGE_BANK[s]][:, 0:128]
+                               ).then_inc(T.sem["m%d" % s], 1)
+            elif op[0] == "C":
+                s = op[1]
+                wait(ve, "v", "m%d" % s, 3)
+                ve.tensor_copy(out=T.cm[:, s * 128:(s + 1) * 128], in_=banks[MERGE_BANK[s]][:, 128:256]
+                               ).then_inc(T.sem["m%d" % s], 1)
+            else:
+                (i, c0, wd, k), st = op[1], op[2]
+                wait(ve, "v", "u%d" % i, 2 * st - 1)
+                if st < LAST:
+                    ve.tensor_tensor(out=hbuf(st)[:, c0:c0 + wd], in0=banks[i % 4][:, 0:wd], in1=T.zeros[:, 0:wd],
+                                     op=AluOpType.max).then_inc(T.sem["u%d" % i], 1)
+                else:
+                    ve.tensor_copy(out=T.yin[:, c0:c0 + wd], in_=banks[i % 4][:, 0:wd]).then_inc(T.sem["u%d" % i], 1)
+
+        if core != sink:
+            for (k, b0, nb, wave) in waves:
+                for u in wave:
+                    wait(g, "g", "u%d" % u[0], 2 * LAST)
+                send([sink], T.yin[:, b0 * TK:(b0 + nb) * TK], "r%d" % k)
+        else:
+            ns = 0
+            for (k, b0, nb, wave) in waves:
+                for u in wave:
+                    wait(g.sync, "s", "u%d" % u[0], 2 * LAST)
+                for m in range(b0, b0 + nb):
+                    g.sync.dma_start(T.y[m], T.yin[:, m * TK:(m + 1) * TK]).then_inc(T.sem.sts, 16)
+                    ns += 16
+            wait(g.sync, "s", "sts", ns)
+            nc = 0
+            for k, (l2, b0, nb) in enumerate(GROUPS):
+                if l2 == ln:
+                    continue
+                wait(g.scalar, "c", "r%d" % k, _count(engines(lanes[l2], [sink])))
+                for m in range(b0, b0 + nb):
+                    g.scalar.dma_start(T.y[m], T.yin[:, m * TK:(m + 1) * TK]).then_inc(T.sem.stc, 16)
+                    nc += 16
+            wait(g.scalar, "c", "stc", nc)
+
+    if sent[0]:
+        wait(g, "g", "snd", sent[0])

@@ -4,9 +4,11 @@ from concourse.mybir import AluOpType
 NR, NB, TK = 6, 8, 256
 LAST = 6
 
-GROUPS = [(0, 0, 2), (1, 2, 2), (0, 4, 2), (1, 6, 1), (0, 7, 1)]
-PRE = {0: 2, 1: 1}
-MERGE_BANK = {0: 4, 1: 5, 3: 6, 4: 7, 2: 4}
+GROUPS = [(0, 0, 2), (1, 2, 2), (0, 4, 2), (2, 6, 2)]
+SKEW = {0: [0, 0, 0, 0], 1: [0, 0], 2: [0, 0]}
+RELAY_ORDER = [2, 1, 0]
+MERGE_BANK = {4: 5, 0: 6, 1: 7, 3: 5, 2: 6}
+BANK_AFTER = {3: 4, 2: 0}
 
 SCRATCH = {
     "wt": ("sbuf", [128, NR * 256], "bfloat16"),
@@ -26,8 +28,8 @@ for _b in range(8):
     SCRATCH["ps%d" % _b] = ("psum", [128, 512], "float32")
 
 SEMAPHORES = (["w%d" % s for s in range(NR)] + ["x%d" % m for m in range(NB)] + ["u%d" % i for i in range(NB)]
-              + ["m%d" % s for s in range(5)] + ["a%d" % k for k in range(len(GROUPS))]
-              + ["r%d" % k for k in range(len(GROUPS))] + ["zs", "ids", "id1", "id2", "snd", "sts", "stc"])
+              + ["q%d" % i for i in range(NB)] + ["m%d" % s for s in range(5)] + ["a%d" % k for k in range(NB)]
+              + ["r%d" % k for k in range(NB)] + ["zs", "ids", "id1", "id2", "snd", "sts", "stc"])
 
 
 def _pick(mask, n):
@@ -51,7 +53,7 @@ def rank_program(g, core, T, topo):
     cores = list(T.cores)
     sink = cores[NR - 1]
     helper = [c for c in cores if c != sink and topo.chip(c) == topo.chip(sink)][0]
-    lanes = [sink, helper]
+    lanes = [sink, helper, cores[0], cores[1]][:1 + max(l for l, _, _ in GROUPS)]
 
     waited = {}
 
@@ -94,20 +96,14 @@ def rank_program(g, core, T, topo):
     def wcols(s):
         return T.wt[:, s * 256 + 128:(s + 1) * 256] if s == 0 else T.wt[:, s * 256:(s + 1) * 256]
 
-    def n_direct(o, direct):
-        return _count(engines(o, direct))
-
-    def n_relay_in(o, relay):
-        return _count(engines(o, [relay], 8))
-
     def w_val(c, s):
         o, direct, blocked, relay = route(s)
         if c == o:
             return 32
         if c in direct:
-            return n_direct(o, direct)
+            return _count(engines(o, direct))
         if c == relay:
-            return n_relay_in(o, relay)
+            return _count(engines(o, [relay], 8))
         return _count(engines(relay, [c]))
 
     g.sync.dma_start(T.wt[:, rank * 256:rank * 256 + 128], T.w1[:, :]).then_inc(T.sem["w%d" % rank], 16)
@@ -123,70 +119,68 @@ def rank_program(g, core, T, topo):
         o2, d2, b2, r2 = route(s)
         if r2 == core:
             wait(g, "g", "w%d" % s, w_val(core, s))
-            for l in b2:
+            for l in [lanes[j] for j in RELAY_ORDER if j < len(lanes) and lanes[j] in b2]:
                 send([l], wcols(s), "w%d" % s)
 
     banks = [T["ps%d" % b] for b in range(8)]
 
-    if rank == 0:
+    if core in lanes:
+        g.vector.memset(T.idsrc[:, :], 0.0).then_inc(T.sem.ids, 1)
+        wait(g.vector, "v", "ids", 1)
+        g.vector.memset(T.idsrc[:, 0:1], 1.0).then_inc(T.sem.ids, 1)
+        wait(g.sync, "s", "ids", 2)
+        g.sync.dma_start(T.idd[:], T.idsrc[:, :]).then_inc(T.sem.id1, 16)
+    if core in lanes or rank == 0:
         g.vector.memset(T.zeros[:, :], 0.0).then_inc(T.sem.zs, 1)
         wait(g.vector, "v", "zs", 1)
+
+    if rank == 0:
         for m in range(NB):
             q = g.sync if m % 2 == 0 else g.scalar
             q.dma_start(T.xin[:, m * TK:(m + 1) * TK], T.x[m]).then_inc(T.sem["x%d" % m], 16)
         wait(g.tensor, "t", "w0", 32)
+        hb0 = [2, 3, 4]
         for m in range(NB):
+            bk = banks[hb0[m % 3]]
             wait(g.tensor, "t", "x%d" % m, 16)
-            g.tensor.matmul(out=banks[m][:, 0:TK], lhsT=T.wt[:, 0:128], rhs=T.xin[:, m * TK:(m + 1) * TK],
-                            start=True, stop=True).then_inc(T.sem["u%d" % m], 1)
-            wait(g.vector, "v", "u%d" % m, 1)
-            g.vector.tensor_tensor(out=T.hin[:, m * TK:(m + 1) * TK], in0=banks[m][:, 0:TK], in1=T.zeros[:, :],
-                                   op=AluOpType.max).then_inc(T.sem["u%d" % m], 1)
+            if m >= 3:
+                wait(g.tensor, "t", "q%d" % (m - 3), 2)
+            g.tensor.matmul(out=bk[:, 0:TK], lhsT=T.wt[:, 0:128], rhs=T.xin[:, m * TK:(m + 1) * TK],
+                            start=True, stop=True).then_inc(T.sem["q%d" % m], 1)
+            wait(g.vector, "v", "q%d" % m, 1)
+            g.vector.tensor_tensor(out=T.hin[:, m * TK:(m + 1) * TK], in0=bk[:, 0:TK], in1=T.zeros[:, :],
+                                   op=AluOpType.max).then_inc(T.sem["q%d" % m], 1)
         for k, (ln, b0, nb) in enumerate(GROUPS):
+            if lanes[ln] == core:
+                continue
             for m in range(b0, b0 + nb):
-                wait(g, "g", "u%d" % m, 2)
+                wait(g, "g", "q%d" % m, 2)
             send([lanes[ln]], T.hin[:, b0 * TK:(b0 + nb) * TK], "a%d" % k)
 
     if core in lanes:
         ln = lanes.index(core)
         src0 = cores[0]
-        waves, i = [], 0
+        units, outs = [], []
         for k, (l2, b0, nb) in enumerate(GROUPS):
             if l2 != ln:
                 continue
-            if nb == 1:
-                cuts = [(b0 * TK, TK // 2), (b0 * TK + TK // 2, TK // 2)]
-            else:
-                cuts = [((b0 + j) * TK, TK) for j in range(nb)]
-            wave = []
-            for (c0, wd) in cuts:
-                wave.append((i, c0, wd, k))
-                i += 1
-            waves.append((k, b0, nb, wave))
-        pre = PRE[ln]
-
-        g.vector.memset(T.idsrc[:, :], 0.0).then_inc(T.sem.ids, 1)
-        wait(g.vector, "v", "ids", 1)
-        g.vector.memset(T.idsrc[:, 0:1], 1.0).then_inc(T.sem.ids, 1)
-        g.vector.memset(T.zeros[:, :], 0.0).then_inc(T.sem.zs, 1)
-        wait(g.vector, "v", "zs", 1)
-        wait(g.sync, "s", "ids", 2)
-        g.sync.dma_start(T.idd[:], T.idsrc[:, :]).then_inc(T.sem.id1, 16)
+            us = [(len(units) + j, (b0 + j) * TK, TK, k) for j in range(nb)]
+            units += us
+            outs.append((k, b0, nb, us))
+        skew = SKEW[ln]
         wait(g.sync, "s", "id1", 16)
         g.sync.dma_start(T.ident[:, :], T.idd[0:128 * 128]).then_inc(T.sem.id2, 16)
 
-        def stages(wave, ks):
-            return [("S", u, k) for k in ks for u in wave]
+        def rnd(r):
+            return [("S", u, r - skew[u[0]]) for u in units if 1 <= r - skew[u[0]] <= LAST]
 
-        w0 = waves[0][3]
-        head = [("T", 4), ("T", 0), ("T", 1), ("C", 4), ("C", 0)] + stages(w0, [1]) + [("T", 3), ("C", 3)]
-        for wv in waves[1:pre]:
-            head += stages(wv[3], [1])
-        tail = [("S", u, 2) for u in w0[1:]] + [("C", 2)] + stages(w0, range(3, LAST + 1))
-        for j, wv in enumerate(waves[1:], 1):
-            tail += stages(wv[3], range(2 if j < pre else 1, LAST + 1))
-        pe_ops = head + [("C", 1), ("T", 2), ("S", w0[0], 2)] + tail
-        ve_ops = head + [("C", 1), ("S", w0[0], 2), ("T", 2)] + tail
+        head = [("T", 4), ("T", 0), ("T", 1), ("C", 4), ("C", 0)] + rnd(1) + [("T", 3), ("C", 3)]
+        r2 = rnd(2)
+        tail = r2[1:] + [("C", 2)]
+        for r in range(3, LAST + 1 + max(skew)):
+            tail += rnd(r)
+        pe_ops = head + [("C", 1), ("T", 2), r2[0]] + tail
+        ve_ops = head + [("C", 1), r2[0], ("T", 2)] + tail
 
         def hbuf(k):
             return T.hin if k == 0 else (T.yin if k == LAST else (T.ha if k % 2 else T.hb))
@@ -197,8 +191,8 @@ def rank_program(g, core, T, topo):
                 s = op[1]
                 wait(pe, "t", "id2", 16)
                 wait(pe, "t", "w%d" % s, w_val(core, s))
-                if s == 2:
-                    wait(pe, "t", "m0", 4)
+                if s in BANK_AFTER:
+                    wait(pe, "t", "m%d" % BANK_AFTER[s], 4)
                 pe.matmul(out=banks[MERGE_BANK[s]][:, 0:128], lhsT=T.wt[:, s * 256 + 128:s * 256 + 256],
                           rhs=T.ident[:, :], start=True, stop=True).then_inc(T.sem["m%d" % s], 1)
             elif op[0] == "C":
@@ -211,9 +205,10 @@ def rank_program(g, core, T, topo):
             else:
                 (i, c0, wd, k), st = op[1], op[2]
                 if st == 1:
-                    wait(pe, "t", "a%d" % k, _count(engines(src0, [core])))
-                    if i >= 4:
-                        wait(pe, "t", "u%d" % (i - 4), 2 * LAST)
+                    if core == src0:
+                        wait(pe, "t", "q%d" % (c0 // TK), 2)
+                    else:
+                        wait(pe, "t", "a%d" % k, _count(engines(src0, [core])))
                 else:
                     wait(pe, "t", "u%d" % i, 2 * (st - 1))
                 if st < LAST:
@@ -222,7 +217,7 @@ def rank_program(g, core, T, topo):
                 else:
                     wait(pe, "t", "w%d" % (NR - 1), w_val(core, NR - 1))
                     lhsT = T.wt[:, (NR - 1) * 256 + 128:NR * 256]
-                pe.matmul(out=banks[i % 4][:, 0:wd], lhsT=lhsT, rhs=hbuf(st - 1)[:, c0:c0 + wd], start=True, stop=True
+                pe.matmul(out=banks[i][:, 0:wd], lhsT=lhsT, rhs=hbuf(st - 1)[:, c0:c0 + wd], start=True, stop=True
                           ).then_inc(T.sem["u%d" % i], 1)
         for op in ve_ops:
             if op[0] == "T":
@@ -239,22 +234,22 @@ def rank_program(g, core, T, topo):
                 (i, c0, wd, k), st = op[1], op[2]
                 wait(ve, "v", "u%d" % i, 2 * st - 1)
                 if st < LAST:
-                    ve.tensor_tensor(out=hbuf(st)[:, c0:c0 + wd], in0=banks[i % 4][:, 0:wd], in1=T.zeros[:, 0:wd],
+                    ve.tensor_tensor(out=hbuf(st)[:, c0:c0 + wd], in0=banks[i][:, 0:wd], in1=T.zeros[:, 0:wd],
                                      op=AluOpType.max).then_inc(T.sem["u%d" % i], 1)
                 else:
-                    ve.tensor_copy(out=T.yin[:, c0:c0 + wd], in_=banks[i % 4][:, 0:wd]).then_inc(T.sem["u%d" % i], 1)
+                    ve.tensor_copy(out=T.yin[:, c0:c0 + wd], in_=banks[i][:, 0:wd]).then_inc(T.sem["u%d" % i], 1)
 
         if core != sink:
-            for (k, b0, nb, wave) in waves:
-                for u in wave:
+            for (k, b0, nb, us) in outs:
+                for u in us:
                     wait(g, "g", "u%d" % u[0], 2 * LAST)
                 send([sink], T.yin[:, b0 * TK:(b0 + nb) * TK], "r%d" % k)
         else:
             ns = 0
-            for (k, b0, nb, wave) in waves:
-                for u in wave:
+            for (k, b0, nb, us) in outs:
+                for u in us:
                     wait(g.sync, "s", "u%d" % u[0], 2 * LAST)
-                for m in range(b0, b0 + nb):
+                    m = u[1] // TK
                     g.sync.dma_start(T.y[m], T.yin[:, m * TK:(m + 1) * TK]).then_inc(T.sem.sts, 16)
                     ns += 16
             wait(g.sync, "s", "sts", ns)

@@ -5,7 +5,8 @@ NR, NB, TK = 6, 8, 256
 LAST = 6
 
 GROUPS = [(0, 0, 2), (1, 2, 2), (0, 4, 2), (2, 6, 2)]
-SKEW = {0: [0, 0, 0, 0], 1: [0, 0], 2: [0, 0]}
+UNITW = {0: 256, 1: 128, 2: 128}
+ONCE = [3]
 RELAY_ORDER = [2, 1, 0]
 MERGE_BANK = {4: 5, 0: 6, 1: 7, 3: 5, 2: 6}
 BANK_AFTER = {3: 4, 2: 0}
@@ -86,6 +87,8 @@ def rank_program(g, core, T, topo):
         o = cores[s]
         direct = [l for l in lanes if l != o and topo.may_write(o, l)]
         blocked = [l for l in lanes if l != o and not topo.may_write(o, l)]
+        if s in ONCE and sink in direct:
+            direct = [l for l in direct if l == sink or topo.chip(l) != topo.chip(sink)]
         relay = None
         if blocked:
             near = [c for c in cores if c != o and topo.chip(c) == topo.chip(o)
@@ -104,6 +107,8 @@ def rank_program(g, core, T, topo):
             return _count(engines(o, direct))
         if c == relay:
             return _count(engines(o, [relay], 8))
+        if s in ONCE and c not in blocked:
+            return _count(engines(sink, [c], 8))
         return _count(engines(relay, [c]))
 
     g.sync.dma_start(T.wt[:, rank * 256:rank * 256 + 128], T.w1[:, :]).then_inc(T.sem["w%d" % rank], 16)
@@ -121,6 +126,12 @@ def rank_program(g, core, T, topo):
             wait(g, "g", "w%d" % s, w_val(core, s))
             for l in [lanes[j] for j in RELAY_ORDER if j < len(lanes) and lanes[j] in b2]:
                 send([l], wcols(s), "w%d" % s)
+    if core == sink:
+        for s in ONCE:
+            near = [l for l in lanes if l != sink and l != cores[s] and topo.chip(l) == topo.chip(sink)]
+            wait(g, "g", "w%d" % s, w_val(core, s))
+            for l in near:
+                send([l], wcols(s), "w%d" % s, 8)
 
     banks = [T["ps%d" % b] for b in range(8)]
 
@@ -161,32 +172,30 @@ def rank_program(g, core, T, topo):
         ln = lanes.index(core)
         src0 = cores[0]
         units, outs = [], []
+        wd0 = UNITW[ln]
         for k, (l2, b0, nb) in enumerate(GROUPS):
             if l2 != ln:
                 continue
-            us = [(len(units) + j, (b0 + j) * TK, TK, k) for j in range(nb)]
+            us = [(len(units) + j, b0 * TK + j * wd0, wd0, k) for j in range(nb * (TK // wd0))]
             units += us
             outs.append((k, b0, nb, us))
-        skew = SKEW[ln]
         wait(g.sync, "s", "id1", 16)
         g.sync.dma_start(T.ident[:, :], T.idd[0:128 * 128]).then_inc(T.sem.id2, 16)
 
         def rnd(r):
-            return [("S", u, r - skew[u[0]]) for u in units if 1 <= r - skew[u[0]] <= LAST]
+            return [("S", u, r) for u in units]
 
-        head = [("T", 4), ("T", 0), ("T", 1), ("C", 4), ("C", 0)] + rnd(1) + [("T", 3), ("C", 3)]
         r2 = rnd(2)
-        tail = r2[1:] + [("C", 2)]
-        for r in range(3, LAST + 1 + max(skew)):
-            tail += rnd(r)
-        pe_ops = head + [("C", 1), ("T", 2), r2[0]] + tail
-        ve_ops = head + [("C", 1), r2[0], ("T", 2)] + tail
+        ops = [("T", 4), ("T", 0), ("T", 1), ("C", 4), ("C", 0), ("T", 3), ("C", 3)] + rnd(1)
+        ops += [("C", 1), ("T", 2)] + r2[:2] + [("C", 2)] + r2[2:]
+        for r in range(3, LAST + 1):
+            ops += rnd(r)
 
         def hbuf(k):
             return T.hin if k == 0 else (T.yin if k == LAST else (T.ha if k % 2 else T.hb))
 
         pe, ve = g.tensor, g.vector
-        for op in pe_ops:
+        for op in ops:
             if op[0] == "T":
                 s = op[1]
                 wait(pe, "t", "id2", 16)
@@ -206,7 +215,8 @@ def rank_program(g, core, T, topo):
                 (i, c0, wd, k), st = op[1], op[2]
                 if st == 1:
                     if core == src0:
-                        wait(pe, "t", "q%d" % (c0 // TK), 2)
+                        for m in range(NB):
+                            wait(pe, "t", "q%d" % m, 2)
                     else:
                         wait(pe, "t", "a%d" % k, _count(engines(src0, [core])))
                 else:
@@ -219,7 +229,7 @@ def rank_program(g, core, T, topo):
                     lhsT = T.wt[:, (NR - 1) * 256 + 128:NR * 256]
                 pe.matmul(out=banks[i][:, 0:wd], lhsT=lhsT, rhs=hbuf(st - 1)[:, c0:c0 + wd], start=True, stop=True
                           ).then_inc(T.sem["u%d" % i], 1)
-        for op in ve_ops:
+        for op in ops:
             if op[0] == "T":
                 s = op[1]
                 wait(ve, "v", "m%d" % s, 1)
@@ -247,9 +257,10 @@ def rank_program(g, core, T, topo):
         else:
             ns = 0
             for (k, b0, nb, us) in outs:
-                for u in us:
-                    wait(g.sync, "s", "u%d" % u[0], 2 * LAST)
-                    m = u[1] // TK
+                for m in range(b0, b0 + nb):
+                    for u in us:
+                        if u[1] // TK == m:
+                            wait(g.sync, "s", "u%d" % u[0], 2 * LAST)
                     g.sync.dma_start(T.y[m], T.yin[:, m * TK:(m + 1) * TK]).then_inc(T.sem.sts, 16)
                     ns += 16
             wait(g.sync, "s", "sts", ns)

@@ -4,12 +4,14 @@ from concourse.mybir import AluOpType
 NR, NB, TK = 6, 8, 256
 LAST = 6
 
-GROUPS = [(0, 0, 2), (1, 2, 2), (0, 4, 2), (2, 6, 2)]
-UNITW = {0: 256, 1: 128, 2: 128}
-ONCE = [3]
-RELAY_ORDER = [2, 1, 0]
-MERGE_BANK = {4: 5, 0: 6, 1: 7, 3: 5, 2: 6}
-BANK_AFTER = {3: 4, 2: 0}
+GROUPS = [(1, 0, 2), (3, 2, 2), (0, 4, 3), (2, 7, 1)]
+UNITW = {0: 256, 1: 128, 2: 64, 3: 128}
+VIA = {3: {1: 0, 2: 3}, 2: {2: 3}}
+RELAY_ORDER = [3, 1, 0]
+DIRECT_ORDER = [1, 2, 3, 0]
+OTHER_ENGINES = [1, 2]
+MERGE_BANK = {0: 6, 1: 7, 4: 5, 3: 4, 2: 6}
+BANK_AFTER = {2: 0}
 
 SCRATCH = {
     "wt": ("sbuf", [128, NR * 256], "bfloat16"),
@@ -19,28 +21,18 @@ SCRATCH = {
     "hb": ("sbuf", [128, NB * TK], "bfloat16"),
     "yin": ("sbuf", [128, NB * TK], "bfloat16"),
     "zeros": ("sbuf", [128, TK], "float32"),
-    "idsrc": ("sbuf", [128, 129], "bfloat16"),
-    "idd": ("dram", [129 * 128], "bfloat16"),
+    "iot": ("sbuf", [128, 128], "float32"),
     "ident": ("sbuf", [128, 128], "bfloat16"),
     "wtr": ("sbuf", [128, 5 * 128], "bfloat16"),
     "cm": ("sbuf", [128, 5 * 128], "bfloat16"),
+    "wd": ("dram", [128, 256], "bfloat16"),
 }
 for _b in range(8):
     SCRATCH["ps%d" % _b] = ("psum", [128, 512], "float32")
 
 SEMAPHORES = (["w%d" % s for s in range(NR)] + ["x%d" % m for m in range(NB)] + ["u%d" % i for i in range(NB)]
               + ["q%d" % i for i in range(NB)] + ["m%d" % s for s in range(5)] + ["a%d" % k for k in range(NB)]
-              + ["r%d" % k for k in range(NB)] + ["zs", "ids", "id1", "id2", "snd", "sts", "stc"])
-
-
-def _pick(mask, n):
-    out, b, c = 0, 0, 0
-    while c < n:
-        if (mask >> b) & 1:
-            out |= 1 << b
-            c += 1
-        b += 1
-    return out
+              + ["r%d" % k for k in range(NB)] + ["zs", "ids", "id2", "snd", "sts", "stc"])
 
 
 def _count(mask):
@@ -54,7 +46,7 @@ def rank_program(g, core, T, topo):
     cores = list(T.cores)
     sink = cores[NR - 1]
     helper = [c for c in cores if c != sink and topo.chip(c) == topo.chip(sink)][0]
-    lanes = [sink, helper, cores[0], cores[1]][:1 + max(l for l, _, _ in GROUPS)]
+    lanes = [sink, helper, cores[0], cores[1]]
 
     waited = {}
 
@@ -66,34 +58,45 @@ def rank_program(g, core, T, topo):
 
     sent = [0]
 
-    def engines(src, dsts, n=None):
-        m = topo.mask(src, dsts[0])
-        for d in dsts[1:]:
-            m &= topo.mask(src, d)
-        return m if n is None else _pick(m, min(n, _count(m)))
+    def eng(src, dst, full=False):
+        m = topo.mask(src, dst)
+        if full or topo.chip(src) != topo.chip(dst):
+            return m
+        far = [c for c in cores if topo.chip(c) != topo.chip(src)][0]
+        if src in [lanes[j] for j in OTHER_ENGINES]:
+            return m & ~topo.mask(src, far)
+        return m & topo.mask(src, far)
 
-    def send(dsts, ap, sem, n=None):
-        m = engines(core, dsts, n)
+    def put(dsts, ap, sem, src=None, full=False):
+        order, by = [], {}
+        for d in dsts:
+            m = eng(core, d, full)
+            if m not in by:
+                by[m] = []
+                order.append(m)
+            by[m].append(d)
+        s_ap = ap if src is None else src
         if len(dsts) == 1:
             rid, pid, _ = topo.addr(dsts[0])
-            g.remote_dma(ap, ap, T.sem[sem], T.sem.snd, pid, rid, m)
+            g.remote_dma(ap, s_ap, T.sem[sem], T.sem.snd, pid, rid, order[0])
         else:
-            ids = [DstId(rid=topo.addr(d)[0], pnc=topo.addr(d)[1]) for d in dsts]
-            g.remote_dma_fused([RemoteDMATransfer(dst_ids=ids, dma_engine_mask=m, remote_sem=T.sem[sem], srcs=[ap],
-                                                  dsts=[ap for _ in dsts])], local_sem=T.sem.snd)
-        sent[0] += _count(m)
+            trs = [RemoteDMATransfer(dst_ids=[DstId(rid=topo.addr(d)[0], pnc=topo.addr(d)[1]) for d in by[m]],
+                                     dma_engine_mask=m, remote_sem=T.sem[sem], srcs=[s_ap],
+                                     dsts=[ap for _ in by[m]]) for m in order]
+            g.remote_dma_fused(trs, local_sem=T.sem.snd)
+        sent[0] += sum(_count(m) for m in order)
 
     def route(s):
         o = cores[s]
-        direct = [l for l in lanes if l != o and topo.may_write(o, l)]
-        blocked = [l for l in lanes if l != o and not topo.may_write(o, l)]
-        if s in ONCE and sink in direct:
-            direct = [l for l in direct if l == sink or topo.chip(l) != topo.chip(sink)]
+        via = VIA.get(s, {})
+        order = DIRECT_ORDER if not via else range(len(lanes))
+        tg = [lanes[j] for j in order if lanes[j] != o and j not in via]
+        direct = [l for l in tg if topo.may_write(o, l)]
+        blocked = [l for l in tg if not topo.may_write(o, l)]
         relay = None
         if blocked:
-            near = [c for c in cores if c != o and topo.chip(c) == topo.chip(o)
-                    and all(topo.may_write(c, l) for l in blocked)]
-            relay = near[0]
+            relay = [c for c in cores if c != o and topo.chip(c) == topo.chip(o)
+                     and all(topo.may_write(c, l) for l in blocked)][0]
         return o, direct, blocked, relay
 
     def wcols(s):
@@ -103,70 +106,100 @@ def rank_program(g, core, T, topo):
         o, direct, blocked, relay = route(s)
         if c == o:
             return 32
-        if c in direct:
-            return _count(engines(o, direct))
-        if c == relay:
-            return _count(engines(o, [relay], 8))
-        if s in ONCE and c not in blocked:
-            return _count(engines(sink, [c], 8))
-        return _count(engines(relay, [c]))
+        if c == relay or c in direct:
+            return _count(eng(o, c))
+        if c in blocked:
+            return _count(eng(relay, c))
+        return _count(eng(lanes[VIA[s][lanes.index(c)]], c))
 
-    g.sync.dma_start(T.wt[:, rank * 256:rank * 256 + 128], T.w1[:, :]).then_inc(T.sem["w%d" % rank], 16)
-    g.scalar.dma_start(T.wt[:, rank * 256 + 128:rank * 256 + 256], T.w2[:, :]).then_inc(T.sem["w%d" % rank], 16)
-
-    o, direct, blocked, relay = route(rank)
-    wait(g, "g", "w%d" % rank, 32)
-    if direct:
-        send(direct, wcols(rank), "w%d" % rank)
-    if blocked:
-        send([relay], wcols(rank), "w%d" % rank, 8)
-    for s in range(NR):
-        o2, d2, b2, r2 = route(s)
-        if r2 == core:
-            wait(g, "g", "w%d" % s, w_val(core, s))
-            for l in [lanes[j] for j in RELAY_ORDER if j < len(lanes) and lanes[j] in b2]:
-                send([l], wcols(s), "w%d" % s)
-    if core == sink:
-        for s in ONCE:
-            near = [l for l in lanes if l != sink and l != cores[s] and topo.chip(l) == topo.chip(sink)]
-            wait(g, "g", "w%d" % s, w_val(core, s))
-            for l in near:
-                send([l], wcols(s), "w%d" % s, 8)
-
-    banks = [T["ps%d" % b] for b in range(8)]
+    def forwards():
+        for s in sorted(VIA, reverse=True):
+            near = [lanes[j] for j in VIA[s] if lanes[VIA[s][j]] == core]
+            if near:
+                wait(g, "g", "w%d" % s, w_val(core, s))
+                put(near, wcols(s), "w%d" % s)
 
     if core in lanes:
-        g.vector.memset(T.idsrc[:, :], 0.0).then_inc(T.sem.ids, 1)
-        wait(g.vector, "v", "ids", 1)
-        g.vector.memset(T.idsrc[:, 0:1], 1.0).then_inc(T.sem.ids, 1)
-        wait(g.sync, "s", "ids", 2)
-        g.sync.dma_start(T.idd[:], T.idsrc[:, :]).then_inc(T.sem.id1, 16)
-    if core in lanes or rank == 0:
-        g.vector.memset(T.zeros[:, :], 0.0).then_inc(T.sem.zs, 1)
-        wait(g.vector, "v", "zs", 1)
+        g.iota(out=T.iot[:, :], pattern=[[-1, 128]], base=0, channel_multiplier=1,
+               allow_small_or_imprecise_dtypes=True).then_inc(T.sem.ids, 1)
 
+    o, direct, blocked, relay = route(rank)
+    wn = "w%d" % rank
+    if blocked:
+        g.sync.dma_start(T.wd[:, 0:128], T.w1[:, :]).then_inc(T.sem[wn], 16)
+        g.scalar.dma_start(T.wd[:, 128:256], T.w2[:, :]).then_inc(T.sem[wn], 16)
+    else:
+        g.sync.dma_start(T.wt[:, rank * 256:rank * 256 + 128], T.w1[:, :]).then_inc(T.sem[wn], 16)
+        g.scalar.dma_start(T.wt[:, rank * 256 + 128:rank * 256 + 256], T.w2[:, :]).then_inc(T.sem[wn], 16)
     if rank == 0:
         for m in range(NB):
             q = g.sync if m % 2 == 0 else g.scalar
             q.dma_start(T.xin[:, m * TK:(m + 1) * TK], T.x[m]).then_inc(T.sem["x%d" % m], 16)
-        wait(g.tensor, "t", "w0", 32)
+
+    wait(g, "g", wn, 32)
+    later = []
+    if rank == 0:
+        later = [l for l in direct if topo.chip(l) == topo.chip(core)]
+        direct = [l for l in direct if l not in later]
+    if direct:
+        put(direct, wcols(rank), wn)
+    if blocked:
+        put([relay], T.wd[:, :], wn)
+    for s in range(NR):
+        o2, d2, b2, r2 = route(s)
+        if r2 == core:
+            wait(g, "g", "w%d" % s, w_val(core, s))
+            for l in [lanes[j] for j in RELAY_ORDER if lanes[j] in b2]:
+                put([l], wcols(s), "w%d" % s, src=T.wd[:, :])
+    forwards()
+
+    banks = [T["ps%d" % b] for b in range(8)]
+    pe, ve = g.tensor, g.vector
+
+    def transpose_pe(s):
+        wait(pe, "t", "id2", 1)
+        wait(pe, "t", "w%d" % s, w_val(core, s))
+        if s in BANK_AFTER:
+            wait(pe, "t", "m%d" % BANK_AFTER[s], 4)
+        pe.matmul(out=banks[MERGE_BANK[s]][:, 0:128], lhsT=T.wt[:, s * 256 + 128:s * 256 + 256],
+                  rhs=T.ident[:, :], start=True, stop=True).then_inc(T.sem["m%d" % s], 1)
+
+    def transpose_ve(s):
+        wait(ve, "v", "m%d" % s, 1)
+        ve.tensor_copy(out=T.wtr[:, s * 128:(s + 1) * 128], in_=banks[MERGE_BANK[s]][:, 0:128]
+                       ).then_inc(T.sem["m%d" % s], 1)
+
+    if core in lanes:
+        ve.memset(T.zeros[:, :], 0.0).then_inc(T.sem.zs, 1)
+        wait(ve, "v", "zs", 1)
+        wait(ve, "v", "ids", 1)
+        ve.tensor_tensor(out=T.ident[:, :], in0=T.iot[:, :], in1=T.zeros[:, 0:128],
+                         op=AluOpType.is_equal).then_inc(T.sem.id2, 1)
+
+    if rank == 0:
+        wait(pe, "t", "w0", 32)
+        transpose_pe(0)
+        transpose_ve(0)
         hb0 = [2, 3, 4]
         for m in range(NB):
             bk = banks[hb0[m % 3]]
-            wait(g.tensor, "t", "x%d" % m, 16)
+            wait(pe, "t", "x%d" % m, 16)
             if m >= 3:
-                wait(g.tensor, "t", "q%d" % (m - 3), 2)
-            g.tensor.matmul(out=bk[:, 0:TK], lhsT=T.wt[:, 0:128], rhs=T.xin[:, m * TK:(m + 1) * TK],
-                            start=True, stop=True).then_inc(T.sem["q%d" % m], 1)
-            wait(g.vector, "v", "q%d" % m, 1)
-            g.vector.tensor_tensor(out=T.hin[:, m * TK:(m + 1) * TK], in0=bk[:, 0:TK], in1=T.zeros[:, :],
-                                   op=AluOpType.max).then_inc(T.sem["q%d" % m], 1)
+                wait(pe, "t", "q%d" % (m - 3), 2)
+            pe.matmul(out=bk[:, 0:TK], lhsT=T.wt[:, 0:128], rhs=T.xin[:, m * TK:(m + 1) * TK],
+                      start=True, stop=True).then_inc(T.sem["q%d" % m], 1)
+            wait(ve, "v", "q%d" % m, 1)
+            ve.tensor_tensor(out=T.hin[:, m * TK:(m + 1) * TK], in0=bk[:, 0:TK], in1=T.zeros[:, :],
+                             op=AluOpType.max).then_inc(T.sem["q%d" % m], 1)
         for k, (ln, b0, nb) in enumerate(GROUPS):
             if lanes[ln] == core:
                 continue
+            if lanes[ln] in later:
+                put(later, wcols(rank), wn)
+                later = []
             for m in range(b0, b0 + nb):
                 wait(g, "g", "q%d" % m, 2)
-            send([lanes[ln]], T.hin[:, b0 * TK:(b0 + nb) * TK], "a%d" % k)
+            put([lanes[ln]], T.hin[:, b0 * TK:(b0 + nb) * TK], "a%d" % k)
 
     if core in lanes:
         ln = lanes.index(core)
@@ -179,31 +212,27 @@ def rank_program(g, core, T, topo):
             us = [(len(units) + j, b0 * TK + j * wd0, wd0, k) for j in range(nb * (TK // wd0))]
             units += us
             outs.append((k, b0, nb, us))
-        wait(g.sync, "s", "id1", 16)
-        g.sync.dma_start(T.ident[:, :], T.idd[0:128 * 128]).then_inc(T.sem.id2, 16)
 
         def rnd(r):
             return [("S", u, r) for u in units]
 
-        r2 = rnd(2)
-        ops = [("T", 4), ("T", 0), ("T", 1), ("C", 4), ("C", 0), ("T", 3), ("C", 3)] + rnd(1)
-        ops += [("C", 1), ("T", 2)] + r2[:2] + [("C", 2)] + r2[2:]
-        for r in range(3, LAST + 1):
+        r2, r3 = rnd(2), rnd(3)
+        if core == sink:
+            ops = [("T", 0), ("T", 1), ("C", 0), ("T", 4), ("T", 3), ("C", 4), ("C", 3)] + rnd(1)
+            ops += [("C", 1), ("T", 2)] + r2[:2] + [("C", 2)] + r2[2:] + r3
+        else:
+            ops = ([] if core == src0 else [("T", 0)]) + [("T", 1), ("C", 0)] + rnd(1) + [("T", 4)]
+            ops += [("C", 1), ("T", 2)] + r2[:2] + [("C", 2)] + r2[2:]
+            ops += [("T", 3)] + r3[:2] + [("C", 3)] + r3[2:] + [("C", 4)]
+        for r in range(4, LAST + 1):
             ops += rnd(r)
 
         def hbuf(k):
             return T.hin if k == 0 else (T.yin if k == LAST else (T.ha if k % 2 else T.hb))
 
-        pe, ve = g.tensor, g.vector
         for op in ops:
             if op[0] == "T":
-                s = op[1]
-                wait(pe, "t", "id2", 16)
-                wait(pe, "t", "w%d" % s, w_val(core, s))
-                if s in BANK_AFTER:
-                    wait(pe, "t", "m%d" % BANK_AFTER[s], 4)
-                pe.matmul(out=banks[MERGE_BANK[s]][:, 0:128], lhsT=T.wt[:, s * 256 + 128:s * 256 + 256],
-                          rhs=T.ident[:, :], start=True, stop=True).then_inc(T.sem["m%d" % s], 1)
+                transpose_pe(op[1])
             elif op[0] == "C":
                 s = op[1]
                 wait(pe, "t", "m%d" % s, 2)
@@ -218,7 +247,7 @@ def rank_program(g, core, T, topo):
                         for m in range(NB):
                             wait(pe, "t", "q%d" % m, 2)
                     else:
-                        wait(pe, "t", "a%d" % k, _count(engines(src0, [core])))
+                        wait(pe, "t", "a%d" % k, _count(eng(src0, core)))
                 else:
                     wait(pe, "t", "u%d" % i, 2 * (st - 1))
                 if st < LAST:
@@ -231,10 +260,7 @@ def rank_program(g, core, T, topo):
                           ).then_inc(T.sem["u%d" % i], 1)
         for op in ops:
             if op[0] == "T":
-                s = op[1]
-                wait(ve, "v", "m%d" % s, 1)
-                ve.tensor_copy(out=T.wtr[:, s * 128:(s + 1) * 128], in_=banks[MERGE_BANK[s]][:, 0:128]
-                               ).then_inc(T.sem["m%d" % s], 1)
+                transpose_ve(op[1])
             elif op[0] == "C":
                 s = op[1]
                 wait(ve, "v", "m%d" % s, 3)
@@ -253,7 +279,7 @@ def rank_program(g, core, T, topo):
             for (k, b0, nb, us) in outs:
                 for u in us:
                     wait(g, "g", "u%d" % u[0], 2 * LAST)
-                send([sink], T.yin[:, b0 * TK:(b0 + nb) * TK], "r%d" % k)
+                put([sink], T.yin[:, b0 * TK:(b0 + nb) * TK], "r%d" % k, full=True)
         else:
             ns = 0
             for (k, b0, nb, us) in outs:
@@ -268,7 +294,7 @@ def rank_program(g, core, T, topo):
             for k, (l2, b0, nb) in enumerate(GROUPS):
                 if l2 == ln:
                     continue
-                wait(g.scalar, "c", "r%d" % k, _count(engines(lanes[l2], [sink])))
+                wait(g.scalar, "c", "r%d" % k, _count(eng(lanes[l2], sink, True)))
                 for m in range(b0, b0 + nb):
                     g.scalar.dma_start(T.y[m], T.yin[:, m * TK:(m + 1) * TK]).then_inc(T.sem.stc, 16)
                     nc += 16

from concourse.bass import DstId, RemoteDMATransfer
from concourse.mybir import AluOpType

NR, NB, TK = 6, 8, 256
LAST = 6

GROUPS = [(1, 0, 2), (3, 2, 2), (0, 4, 3), (2, 7, 1)]
UNITW = {0: 256, 1: 128, 2: 64, 3: 128}
VIA = {3: {1: 0, 2: 3}, 2: {2: 3}}
RELAY_ORDER = [3, 1, 0]
DIRECT_ORDER = [1, 2, 3, 0]
OTHER_ENGINES = [1, 2]
MERGE_BANK = {0: 6, 1: 7, 4: 5, 3: 4, 2: 6}
BANK_AFTER = {2: 0}

SCRATCH = {
    "wt": ("sbuf", [128, NR * 256], "bfloat16"),
    "xin": ("sbuf", [128, NB * TK], "bfloat16"),
    "hin": ("sbuf", [128, NB * TK], "bfloat16"),
    "ha": ("sbuf", [128, NB * TK], "bfloat16"),
    "hb": ("sbuf", [128, NB * TK], "bfloat16"),
    "yin": ("sbuf", [128, NB * TK], "bfloat16"),
    "zeros": ("sbuf", [128, TK], "float32"),
    "iot": ("sbuf", [128, 128], "float32"),
    "ident": ("sbuf", [128, 128], "bfloat16"),
    "wtr": ("sbuf", [128, 5 * 128], "bfloat16"),
    "cm": ("sbuf", [128, 5 * 128], "bfloat16"),
    "wd": ("dram", [128, 256], "bfloat16"),
}
for _b in range(8):
    SCRATCH["ps%d" % _b] = ("psum", [128, 512], "float32")

SEMAPHORES = (["w%d" % s for s in range(NR)] + ["x%d" % m for m in range(NB)] + ["u%d" % i for i in range(NB)]
              + ["q%d" % i for i in range(NB)] + ["m%d" % s for s in range(5)] + ["a%d" % k for k in range(NB)]
              + ["r%d" % k for k in range(NB)] + ["zs", "ids", "id2", "snd", "sts", "stc"])


def _count(mask):
    return bin(mask).count("1")


def rank_program(g, core, T, topo):
    rank = T.rank_of(core)
    if rank is None:
        return
    cores = list(T.cores)
    sink = cores[NR - 1]
    helper = [c for c in cores if c != sink and topo.chip(c) == topo.chip(sink)][0]
    lanes = [sink, helper, cores[0], cores[1]]

    waited = {}

    def wait(q, qn, name, val):
        if waited.get((qn, name), 0) >= val:
            return
        waited[(qn, name)] = val
        q.wait_ge(T.sem[name], val)

    sent = [0]

    def eng(src, dst, full=False):
        m = topo.mask(src, dst)
        if full or topo.chip(src) != topo.chip(dst):
            return m
        far = [c for c in cores if topo.chip(c) != topo.chip(src)][0]
        if src in [lanes[j] for j in OTHER_ENGINES]:
            return m & ~topo.mask(src, far)
        return m & topo.mask(src, far)

    def put(dsts, ap, sem, src=None, full=False):
        order, by = [], {}
        for d in dsts:
            m = eng(core, d, full)
            if m not in by:
                by[m] = []
                order.append(m)
            by[m].append(d)
        s_ap = ap if src is None else src
        if len(dsts) == 1:
            rid, pid, _ = topo.addr(dsts[0])
            g.remote_dma(ap, s_ap, T.sem[sem], T.sem.snd, pid, rid, order[0])
        else:
            trs = [RemoteDMATransfer(dst_ids=[DstId(rid=topo.addr(d)[0], pnc=topo.addr(d)[1]) for d in by[m]],
                                     dma_engine_mask=m, remote_sem=T.sem[sem], srcs=[s_ap],
                                     dsts=[ap for _ in by[m]]) for m in order]
            g.remote_dma_fused(trs, local_sem=T.sem.snd)
        sent[0] += sum(_count(m) for m in order)

    def route(s):
        o = cores[s]
        via = VIA.get(s, {})
        order = DIRECT_ORDER if not via else range(len(lanes))
        tg = [lanes[j] for j in order if lanes[j] != o and j not in via]
        direct = [l for l in tg if topo.may_write(o, l)]
        blocked = [l for l in tg if not topo.may_write(o, l)]
        relay = None
        if blocked:
            relay = [c for c in cores if c != o and topo.chip(c) == topo.chip(o)
                     and all(topo.may_write(c, l) for l in blocked)][0]
        return o, direct, blocked, relay

    def wcols(s):
        return T.wt[:, s * 256 + 128:(s + 1) * 256] if s == 0 else T.wt[:, s * 256:(s + 1) * 256]

    def w_val(c, s):
        o, direct, blocked, relay = route(s)
        if c == o:
            return 32
        if c == relay or c in direct:
            return _count(eng(o, c))
        if c in blocked:
            return _count(eng(relay, c))
        return _count(eng(lanes[VIA[s][lanes.index(c)]], c))

    def forwards():
        for s in sorted(VIA, reverse=True):
            near = [lanes[j] for j in VIA[s] if lanes[VIA[s][j]] == core]
            if near:
                wait(g, "g", "w%d" % s, w_val(core, s))
                put(near, wcols(s), "w%d" % s)

    if core in lanes:
        g.iota(out=T.iot[:, :], pattern=[[-1, 128]], base=0, channel_multiplier=1,
               allow_small_or_imprecise_dtypes=True).then_inc(T.sem.ids, 1)

    o, direct, blocked, relay = route(rank)
    wn = "w%d" % rank
    if blocked:
        g.sync.dma_start(T.wd[:, 0:128], T.w1[:, :]).then_inc(T.sem[wn], 16)
        g.scalar.dma_start(T.wd[:, 128:256], T.w2[:, :]).then_inc(T.sem[wn], 16)
    else:
        g.sync.dma_start(T.wt[:, rank * 256:rank * 256 + 128], T.w1[:, :]).then_inc(T.sem[wn], 16)
        g.scalar.dma_start(T.wt[:, rank * 256 + 128:rank * 256 + 256], T.w2[:, :]).then_inc(T.sem[wn], 16)
    if rank == 0:
        for m in range(NB):
            q = g.sync if m % 2 == 0 else g.scalar
            q.dma_start(T.xin[:, m * TK:(m + 1) * TK], T.x[m]).then_inc(T.sem["x%d" % m], 16)

    wait(g, "g", wn, 32)
    later = []
    if rank == 0:
        later = [l for l in direct if topo.chip(l) == topo.chip(core)]
        direct = [l for l in direct if l not in later]
    if direct:
        put(direct, wcols(rank), wn)
    if blocked:
        put([relay], T.wd[:, :], wn)
    for s in range(NR):
        o2, d2, b2, r2 = route(s)
        if r2 == core:
            wait(g, "g", "w%d" % s, w_val(core, s))
            for l in [lanes[j] for j in RELAY_ORDER if lanes[j] in b2]:
                put([l], wcols(s), "w%d" % s, src=T.wd[:, :])
    forwards()

    banks = [T["ps%d" % b] for b in range(8)]
    pe, ve = g.tensor, g.vector

    def transpose_pe(s):
        wait(pe, "t", "id2", 1)
        wait(pe, "t", "w%d" % s, w_val(core, s))
        if s in BANK_AFTER:
            wait(pe, "t", "m%d" % BANK_AFTER[s], 4)
        pe.matmul(out=banks[MERGE_BANK[s]][:, 0:128], lhsT=T.wt[:, s * 256 + 128:s * 256 + 256],
                  rhs=T.ident[:, :], start=True, stop=True).then_inc(T.sem["m%d" % s], 1)

    def transpose_ve(s):
        wait(ve, "v", "m%d" % s, 1)
        ve.tensor_copy(out=T.wtr[:, s * 128:(s + 1) * 128], in_=banks[MERGE_BANK[s]][:, 0:128]
                       ).then_inc(T.sem["m%d" % s], 1)

    if core in lanes:
        ve.memset(T.zeros[:, :], 0.0).then_inc(T.sem.zs, 1)
        wait(ve, "v", "zs", 1)
        wait(ve, "v", "ids", 1)
        ve.tensor_tensor(out=T.ident[:, :], in0=T.iot[:, :], in1=T.zeros[:, 0:128],
                         op=AluOpType.is_equal).then_inc(T.sem.id2, 1)

    if rank == 0:
        wait(pe, "t", "w0", 32)
        transpose_pe(0)
        transpose_ve(0)
        hb0 = [2, 3, 4]
        for m in range(NB):
            bk = banks[hb0[m % 3]]
            wait(pe, "t", "x%d" % m, 16)
            if m >= 3:
                wait(pe, "t", "q%d" % (m - 3), 2)
            pe.matmul(out=bk[:, 0:TK], lhsT=T.wt[:, 0:128], rhs=T.xin[:, m * TK:(m + 1) * TK],
                      start=True, stop=True).then_inc(T.sem["q%d" % m], 1)
            wait(ve, "v", "q%d" % m, 1)
            ve.tensor_tensor(out=T.hin[:, m * TK:(m + 1) * TK], in0=bk[:, 0:TK], in1=T.zeros[:, :],
                             op=AluOpType.max).then_inc(T.sem["q%d" % m], 1)
        for k, (ln, b0, nb) in enumerate(GROUPS):
            if lanes[ln] == core:
                continue
            if lanes[ln] in later:
                put(later, wcols(rank), wn)
                later = []
            for m in range(b0, b0 + nb):
                wait(g, "g", "q%d" % m, 2)
            put([lanes[ln]], T.hin[:, b0 * TK:(b0 + nb) * TK], "a%d" % k)

    if core in lanes:
        ln = lanes.index(core)
        src0 = cores[0]
        units, outs = [], []
        wd0 = UNITW[ln]
        for k, (l2, b0, nb) in enumerate(GROUPS):
            if l2 != ln:
                continue
            us = [(len(units) + j, b0 * TK + j * wd0, wd0, k) for j in range(nb * (TK // wd0))]
            units += us
            outs.append((k, b0, nb, us))

        def rnd(r):
            return [("S", u, r) for u in units]

        r2, r3 = rnd(2), rnd(3)
        if core == sink:
            ops = [("T", 0), ("T", 1), ("C", 0), ("T", 4), ("T", 3), ("C", 4), ("C", 3)] + rnd(1)
            ops += [("C", 1), ("T", 2)] + r2[:2] + [("C", 2)] + r2[2:] + r3
        else:
            ops = ([] if core == src0 else [("T", 0)]) + [("T", 1), ("C", 0)] + rnd(1) + [("T", 4)]
            ops += [("C", 1), ("T", 2)] + r2[:2] + [("C", 2)] + r2[2:]
            ops += [("T", 3)] + r3[:2] + [("C", 3)] + r3[2:] + [("C", 4)]
        for r in range(4, LAST + 1):
            ops += rnd(r)

        def hbuf(k):
            return T.hin if k == 0 else (T.yin if k == LAST else (T.ha if k % 2 else T.hb))

        for op in ops:
            if op[0] == "T":
                transpose_pe(op[1])
            elif op[0] == "C":
                s = op[1]
                wait(pe, "t", "m%d" % s, 2)
                wait(pe, "t", "w%d" % (s + 1), w_val(core, s + 1))
                pe.matmul(out=banks[MERGE_BANK[s]][:, 128:256], lhsT=T.wtr[:, s * 128:(s + 1) * 128],
                          rhs=T.wt[:, (s + 1) * 256:(s + 1) * 256 + 128], start=True, stop=True
                          ).then_inc(T.sem["m%d" % s], 1)
            else:
                (i, c0, wd, k), st = op[1], op[2]
                if st == 1:
                    if core == src0:
                        for m in range(NB):
                            wait(pe, "t", "q%d" % m, 2)
                    else:
                        wait(pe, "t", "a%d" % k, _count(eng(src0, core)))
                else:
                    wait(pe, "t", "u%d" % i, 2 * (st - 1))
                if st < LAST:
                    wait(pe, "t", "m%d" % (st - 1), 4)
                    lhsT = T.cm[:, (st - 1) * 128:st * 128]
                else:
                    wait(pe, "t", "w%d" % (NR - 1), w_val(core, NR - 1))
                    lhsT = T.wt[:, (NR - 1) * 256 + 128:NR * 256]
                pe.matmul(out=banks[i][:, 0:wd], lhsT=lhsT, rhs=hbuf(st - 1)[:, c0:c0 + wd], start=True, stop=True
                          ).then_inc(T.sem["u%d" % i], 1)
        for op in ops:
            if op[0] == "T":
                transpose_ve(op[1])
            elif op[0] == "C":
                s = op[1]
                wait(ve, "v", "m%d" % s, 3)
                ve.tensor_copy(out=T.cm[:, s * 128:(s + 1) * 128], in_=banks[MERGE_BANK[s]][:, 128:256]
                               ).then_inc(T.sem["m%d" % s], 1)
            else:
                (i, c0, wd, k), st = op[1], op[2]
                wait(ve, "v", "u%d" % i, 2 * st - 1)
                if st < LAST:
                    ve.tensor_tensor(out=hbuf(st)[:, c0:c0 + wd], in0=banks[i][:, 0:wd], in1=T.zeros[:, 0:wd],
                                     op=AluOpType.max).then_inc(T.sem["u%d" % i], 1)
                else:
                    ve.tensor_copy(out=T.yin[:, c0:c0 + wd], in_=banks[i][:, 0:wd]).then_inc(T.sem["u%d" % i], 1)

        if core != sink:
            for (k, b0, nb, us) in outs:
                for u in us:
                    wait(g, "g", "u%d" % u[0], 2 * LAST)
                put([sink], T.yin[:, b0 * TK:(b0 + nb) * TK], "r%d" % k, full=True)
        else:
            ns = 0
            for (k, b0, nb, us) in outs:
                for m in range(b0, b0 + nb):
                    for u in us:
                        if u[1] // TK == m:
                            wait(g.sync, "s", "u%d" % u[0], 2 * LAST)
                    g.sync.dma_start(T.y[m], T.yin[:, m * TK:(m + 1) * TK]).then_inc(T.sem.sts, 16)
                    ns += 16
            wait(g.sync, "s", "sts", ns)
            nc = 0
            for k, (l2, b0, nb) in enumerate(GROUPS):
                if l2 == ln:
                    continue
                wait(g.scalar, "c", "r%d" % k, _count(eng(lanes[l2], sink, True)))
                for m in range(b0, b0 + nb):
                    g.scalar.dma_start(T.y[m], T.yin[:, m * TK:(m + 1) * TK]).then_inc(T.sem.stc, 16)
                    nc += 16
            wait(g.scalar, "c", "stc", nc)

    if sent[0]:
        wait(g, "g", "snd", sent[0])
